import numpy as np
import ml_dtypes


def mxq(x, axis, fmt="e4m3"):
    dtype, down = {"e4m3": (ml_dtypes.float8_e4m3fn, 7), "e5m2": (ml_dtypes.float8_e5m2, 14)}[fmt]
    v = np.moveaxis(np.asarray(x, np.float32).astype(ml_dtypes.bfloat16).astype(np.float64), axis, -1)
    blocks = v.reshape(v.shape[:-1] + (-1, 32))
    amax = np.abs(blocks).max(-1, keepdims=True)
    byte = np.maximum(np.where(amax > 0, np.frexp(amax)[1] - 1 + 127, 0) - down, 1)
    scale = np.exp2(byte - 127.0)
    codes = (blocks / scale).astype(np.float32).astype(dtype).astype(np.float64)
    return np.moveaxis((codes * scale).reshape(v.shape), -1, axis)


WIDE = False


def mx_kscale(k):
    if not WIDE:
        return np.ones(k)
    levels = np.array([10, -10, 5, -5, 0])
    if k % 512:
        return np.exp2(np.random.permutation(np.resize(levels, k // 32))).repeat(32)
    a = np.empty((k // 512, 16))
    for p in range(k // 512):
        a[p, :8] = np.random.permutation(np.resize(levels, 8))
        for g in range(8):
            far = levels[np.abs(levels - a[p, g]) >= 10]
            a[p, g + 8] = far[np.random.randint(len(far))]
    return np.exp2(a.ravel()).repeat(32)


def f64(x):
    return np.asarray(x).astype(np.float64)


def striped(idx):
    return np.tile(idx.reshape(-1, 16).T, (8, 1)).astype(np.uint16)


def unstriped(offs):
    return offs[:16].T.reshape(-1).astype(np.int64)


def striped8(idx):
    return np.concatenate([x.reshape(-1, 16).T for x in idx]).astype(np.uint16)


def runs(offs, k):
    lists = np.stack([offs[16 * r : 16 * r + 16].T.reshape(-1) for r in range(8)]).astype(np.int64)
    return lists[np.arange(k) % 512 // 64]


def pack_weight(w):
    k, n = w.shape
    w = f64(np.asarray(w, np.float32).astype(ml_dtypes.bfloat16)).reshape(k // 32, 32, n)
    amax = np.abs(w).max(1)
    byte = np.clip(np.where(amax > 0, np.frexp(amax)[1] - 1 + 127 - 7, 1), 1, 254)
    scaled = (w * np.exp2(127.0 - byte)[:, None, :]).reshape(k, n).astype(np.float32)
    words = np.ascontiguousarray(scaled.reshape(k // 512, 128, 4, n).transpose(0, 1, 3, 2)).astype(ml_dtypes.float8_e4m3fn).view(np.uint8)
    return words, np.ascontiguousarray(byte.astype(np.uint8).reshape(k // 512, 16, n))


def unpack_weight(words, scales):
    g, p, n, _ = words.shape
    vals = np.ascontiguousarray(words).view(ml_dtypes.float8_e4m3fn).astype(np.float64) * np.repeat(np.exp2(scales.astype(np.float64) - 127.0), 8, axis=1)[..., None]
    return vals.transpose(0, 1, 3, 2).reshape(g * 512, n)


E2M1 = np.array([0.0, 0.5, 1.0, 1.5, 2.0, 3.0, 4.0, 6.0, -0.0, -0.5, -1.0, -1.5, -2.0, -3.0, -4.0, -6.0])


def pack_fp4(w):
    k, n = w.shape
    w = f64(np.asarray(w, np.float32).astype(ml_dtypes.bfloat16)).reshape(k // 32, 32, n)
    amax = np.abs(w).max(1)
    mant, ex = np.frexp(amax / 6.0)
    byte = np.clip(np.where(amax > 0, np.where(mant > 0.5, ex, ex - 1) + 127, 1), 1, 254)
    scaled = (w * np.exp2(127.0 - byte)[:, None, :]).reshape(k, n).astype(np.float32)
    c = np.ascontiguousarray(scaled.reshape(k // 512, 128, 4, n).transpose(0, 1, 3, 2)).astype(ml_dtypes.float4_e2m1fn).view(np.uint8) & 0xF
    words = (c[..., 0::2] | (c[..., 1::2] << 4)).reshape(k // 512, 128, 2 * n)
    return np.ascontiguousarray(words), np.ascontiguousarray(byte.astype(np.uint8).reshape(k // 512, 16, n))


def unpack_fp4(words, scales):
    g, _, n = scales.shape
    words = np.ascontiguousarray(words).reshape(g, 128, n, 2)
    nib = np.empty((g, 128, n, 4), np.uint8)
    nib[..., 0::2] = words & 0xF
    nib[..., 1::2] = words >> 4
    vals = E2M1[nib] * np.repeat(np.exp2(scales.astype(np.float64) - 127.0), 8, axis=1)[..., None]
    return vals.transpose(0, 1, 3, 2).reshape(g * 512, n)


def relu(v):
    return np.maximum(v, 0.0)

def planes(y):
    n, m = y.shape
    v = y.astype(np.float32).astype(ml_dtypes.bfloat16).astype(np.float64).reshape(n // 32, 32, m)
    top = np.abs(v).max(1)
    byte = np.clip(np.where(top > 0, np.frexp(top)[1] - 1 + 127 - 7, 1), 1, 254)
    codes = (v * np.exp2(127.0 - byte)[:, None, :]).reshape(n, m).astype(np.float32).astype(ml_dtypes.float8_e4m3fn).view(np.uint8)
    words = codes.reshape(n // 512, 128, 4, m).transpose(0, 1, 3, 2)
    return np.ascontiguousarray(words), np.ascontiguousarray(byte.astype(np.uint8).reshape(n // 512, 16, m))


K, T, S, N, H = 512, 2048, 512, 512, 512


def setup_inputs():
    n = np.random.standard_normal
    s = mx_kscale(K)[:, None]
    u = mx_kscale(H)
    packed_xT = pack_weight(n((K, T)) * s)
    packed_w1 = pack_fp4(n((K, H)) / np.sqrt(K) / s)
    packed_w2 = pack_fp4(n((H, N)) / np.sqrt(H) / u[:, None])
    return {
        "x_words": packed_xT[0],
        "x_scales": packed_xT[1],
        "w1_words": packed_w1[0],
        "w1_scales": packed_w1[1],
        "gn": (np.random.uniform(0.5, 1.5, (H, 1)) * u[:, None]).astype(np.float32),
        "w2_words": packed_w2[0],
        "w2_scales": packed_w2[1],
        "offs": striped(np.random.permutation(T)[:S]),
        "x1": striped8(np.stack([np.random.permutation(S) for _ in range(8)])),
        "x2": striped8(np.stack([np.random.permutation(S) for _ in range(8)])),
        "u1": striped8(np.stack([np.random.permutation(S) for _ in range(8)])),
        "u2": striped8(np.stack([np.random.permutation(S) for _ in range(8)])),
    }


def reference(x_words, x_scales, w1_words, w1_scales, gn, w2_words, w2_scales, offs, x1, x2, u1, u2):
    xq = unpack_weight(x_words, x_scales)[:, unstriped(offs)]
    y = unpack_fp4(w1_words, w1_scales).T @ xq
    a = relu(y - (np.minimum(y[np.arange(H)[:, None], runs(x1, H)], y[np.arange(H)[:, None], runs(x2, H)])))
    b = relu(y - (np.minimum(y[np.arange(H)[:, None], runs(u1, H)], y[np.arange(H)[:, None], runs(u2, H)])))
    z = f64(gn) * (np.sqrt((a) ** 2 + (b) ** 2 + 0.05))
    out_0 = unpack_fp4(w2_words, w2_scales).T @ mxq(z, 0, "e4m3")
    return (out_0,) + planes(out_0)

@@ -1,0 +1,213 @@
+from contextlib import ExitStack
+
+import concourse.mybir as mybir
+from concourse.masks import make_identity
+
+K, T, S, H, N = 512, 2048, 512, 512, 512
+FLOPS = 2 * K * H * S + 2 * H * N * S
+
+F32 = mybir.dt.float32
+BF16 = mybir.dt.bfloat16
+I32 = mybir.dt.int32
+U32 = mybir.dt.uint32
+U16 = mybir.dt.uint16
+U8 = mybir.dt.uint8
+FP8X4 = mybir.dt.float8_e4m3fn_x4
+FP4X4 = mybir.dt.float4_e2m1fn_x4
+ALU = mybir.AluOpType
+ACT = mybir.ActivationFunctionType
+
+P = 128
+PACK = 4
+BLOCK = 128
+HALF = S // 2
+CHUNKS = ((0, 256), (256, 128), (384, 128))
+FLOOR = 0.05
+
+
+def load_scale_rows(queue, plane, rows):
+    for q in range(4):
+        queue.dma_start(out=plane[32 * q : 32 * q + 4, :].bitcast(I32), in_=rows[4 * q : 4 * q + 4, :].bitcast(I32))
+
+
+def deal_columns(nc, dealt, raw, width):
+    nc.vector.tensor_copy(
+        out=dealt[:].rearrange("p (t m b) -> p t m b", t=PACK, b=width),
+        in_=raw[:].rearrange("p (m t b) -> p t m b", t=PACK, b=width),
+    )
+
+
+def tile_picked_eikonal_none_po_kernel(
+    tc, x_words, x_scales, w1_words, w1_scales, gn, w2_words, w2_scales, offs, x1, x2, u1, u2, out_0, out_1, out_2
+):
+    nc = tc.nc
+    with ExitStack() as ctx:
+        keep = ctx.enter_context(tc.tile_pool(name="keep", bufs=1))
+        work = ctx.enter_context(tc.tile_pool(name="work", bufs=2))
+        psum = ctx.enter_context(tc.psum_pool(name="psum", bufs=1))
+
+        x_codes = keep.tile([P, T], U32, name="x_codes", align_bytes=64)
+        x_plane = keep.tile([P, T], U8, name="x_plane", align_bytes=64)
+        w1_raw = keep.tile([P, 2 * H], U8, name="w1_raw", align_bytes=64)
+        w1_plane_raw = keep.tile([P, H], U8, name="w1_plane_raw", align_bytes=64)
+        w2_raw = keep.tile([P, 2 * N], U8, name="w2_raw", align_bytes=64)
+        w2_plane_raw = keep.tile([P, N], U8, name="w2_plane_raw", align_bytes=64)
+        gain = keep.tile([P, PACK], F32, name="gain")
+        picks = keep.tile([P, S // 16], U16, name="picks")
+        lists = [keep.tile([P, S // 16], U16, name=name) for name in ("list_x1", "list_u1", "list_x2", "list_u2")]
+        ident = keep.tile([P, P], F32, name="ident", align_bytes=64)
+        warm = keep.tile([P, 1], F32, name="warm")
+
+        nc.vector.memset(x_plane[:].bitcast(I32), 0)
+        nc.vector.memset(w1_plane_raw[:].bitcast(I32), 0)
+        nc.vector.memset(w2_plane_raw[:].bitcast(I32), 0)
+        make_identity(nc, ident[:])
+
+        nc.sync.dma_start(out=w1_raw[:].bitcast(I32), in_=w1_words[0].bitcast(I32))
+        nc.sync.dma_start(picks[:], offs)
+        for tile, source in zip(lists, (x1, u1, x2, u2)):
+            nc.sync.dma_start(tile[:], source)
+        nc.scalar.dma_start(out=gain[:], in_=gn.rearrange("(p t) o -> p (t o)", t=PACK))
+        nc.sync.dma_start(out=x_codes[:].bitcast(I32), in_=x_words[0].rearrange("p n t -> p (n t)").bitcast(I32))
+        load_scale_rows(nc.sync, x_plane, x_scales[0])
+        load_scale_rows(nc.sync, w1_plane_raw, w1_scales[0])
+        nc.gpsimd.dma_start(out=w2_raw[:].bitcast(I32), in_=w2_words[0].bitcast(I32))
+        load_scale_rows(nc.gpsimd, w2_plane_raw, w2_scales[0])
+
+        nc.scalar.activation(out=warm[:], in_=ident[:, 0:1], func=ACT.Sqrt, bias=FLOOR)
+
+        w1_codes = keep.tile([P, 2 * H], U8, name="w1_codes", align_bytes=64)
+        w1_plane = keep.tile([P, H], U8, name="w1_plane", align_bytes=64)
+        w2_codes = keep.tile([P, 2 * N], U8, name="w2_codes", align_bytes=64)
+        w2_plane = keep.tile([P, N], U8, name="w2_plane", align_bytes=64)
+        picked_codes = keep.tile([P, S], U32, name="picked_codes", align_bytes=64)
+        picked_plane = keep.tile([P, S], U8, name="picked_plane", align_bytes=64)
+
+        deal_columns(nc, w1_codes, w1_raw, 2)
+        nc.vector.tensor_copy(out=picked_plane[:], in_=x_plane[:].indirect(picks[:]))
+        deal_columns(nc, w1_plane, w1_plane_raw, 1)
+        for h in range(2):
+            nc.vector.tensor_copy(
+                out=picked_codes[:, h * HALF : (h + 1) * HALF],
+                in_=x_codes[:].indirect(picks[:, h * HALF // 16 : (h + 1) * HALF // 16]),
+            )
+        deal_columns(nc, w2_codes, w2_raw, 2)
+        deal_columns(nc, w2_plane, w2_plane_raw, 1)
+
+        def product(out, codes, plane, t, rhs, rhs_plane):
+            nc.tensor.matmul_mx(
+                out=out,
+                lhsT=codes[:, 2 * P * t : 2 * P * (t + 1)].bitcast(FP4X4),
+                lhsT_scale=plane[:, P * t : P * (t + 1)],
+                rhs=rhs.bitcast(FP8X4),
+                rhs_scale=rhs_plane,
+                start=True,
+                stop=True,
+            )
+
+        y = [keep.tile([P, S], F32, name=f"y{t}", align_bytes=64) for t in range(PACK)]
+        for h in range(2):
+            cols = slice(h * HALF, (h + 1) * HALF)
+            first = psum.tile([P, HALF], F32, name="first", tag="out_bank", bufs=2)
+            product(first[:], w1_codes, w1_plane, 0, picked_codes[:, cols], picked_plane[:, cols])
+            if h == 0:
+                nc.scalar.copy(out=y[0][:, cols], in_=first[:])
+            else:
+                nc.vector.tensor_copy(out=y[0][:, cols], in_=first[:])
+        for t in range(1, PACK):
+            bank = psum.tile([P, S], F32, name="bank", tag="sum_bank", bufs=3)
+            product(bank[:], w1_codes, w1_plane, t, picked_codes[:], picked_plane[:])
+            nc.scalar.copy(out=y[t][:], in_=bank[:])
+
+        out_codes = keep.tile([P, S], U32, name="out_codes", align_bytes=64)
+        out_plane = keep.tile([P, S], U8, name="out_plane", align_bytes=64)
+        out_rows = out_0.rearrange("(p t) j -> p t j", t=PACK)
+        out_words = out_1[0].rearrange("p n t -> p (n t)").bitcast(I32)
+
+        def gather(fetched, t, c0, width, which):
+            nc.vector.tensor_scalar(
+                out=fetched[:, which, :],
+                in0=y[t][:].indirect(lists[which][:, c0 // 16 : (c0 + width) // 16]),
+                scalar1=-1.0,
+                scalar2=0.0,
+                op0=ALU.mult,
+                op1=ALU.add,
+            )
+
+        def slopes(fetched, sums, t, c0, width):
+            blocks = width // BLOCK
+            least = work.tile([P, 2, width], F32, name="least", tag="least", align_bytes=64)
+            nc.vector.tensor_tensor(out=least[:], in0=fetched[:, 0:2, :], in1=fetched[:, 2:4, :], op=ALU.max)
+            diff = psum.tile([P, 2, blocks, P], F32, name="diff", tag="diff_bank", bufs=3)
+            for side in range(2):
+                for b in range(blocks):
+                    cols = slice(c0 + b * BLOCK, c0 + (b + 1) * BLOCK)
+                    nc.tensor.matmul(diff[:, side, b, :], lhsT=y[t][:, cols], rhs=ident[:], start=True, stop=False, is_transpose=True)
+                    nc.tensor.matmul(
+                        diff[:, side, b, :],
+                        lhsT=least[:, side, b * BLOCK : (b + 1) * BLOCK],
+                        rhs=ident[:],
+                        start=False,
+                        stop=True,
+                        is_transpose=True,
+                    )
+            rise = work.tile([P, 2, blocks, P], F32, name="rise", tag="rise", align_bytes=64)
+            nc.scalar.activation(out=rise[:], in_=diff[:], func=ACT.Relu)
+            square = work.tile([P, 2, blocks, P], F32, name="square", tag="square", align_bytes=64)
+            nc.scalar.activation(out=square[:], in_=rise[:], func=ACT.Square)
+            for b in range(blocks):
+                for side in range(2):
+                    nc.tensor.matmul(
+                        sums[b][:, t, :], lhsT=square[:, side, b, :], rhs=ident[:], start=side == 0, stop=side == 1, is_transpose=True
+                    )
+
+        def finish(total, c0):
+            cols = slice(c0, c0 + BLOCK)
+            last = c0 + BLOCK == S
+            root = work.tile([P, BLOCK, PACK], F32, name="root", tag="root", align_bytes=64)
+            nc.scalar.activation(out=root[:], in_=total[:].rearrange("p t j -> p j t"), func=ACT.Sqrt, bias=FLOOR)
+            z = work.tile([P, BLOCK, PACK], BF16, name="z", tag="z", align_bytes=64)
+            nc.vector.tensor_tensor(out=z[:], in0=root[:], in1=gain[:].unsqueeze(1).to_broadcast([P, BLOCK, PACK]), op=ALU.mult)
+            z_codes = work.tile([P, BLOCK], U32, name="z_codes", tag="z_codes", align_bytes=64)
+            z_plane = work.tile([P, BLOCK], U8, name="z_plane", tag="z_plane", align_bytes=64)
+            nc.vector.quantize_mx(out=z_codes[:].bitcast(FP8X4), scales=z_plane[:], in_=z[:].rearrange("p j t -> p (j t)"))
+            result = psum.tile([P, PACK, BLOCK], F32, name="result", tag="out_bank", bufs=2)
+            for t in range(PACK):
+                product(result[:, t, :], w2_codes, w2_plane, t, z_codes[:], z_plane[:])
+            values = work.tile([P, PACK, BLOCK], F32, name="values", tag="values", align_bytes=64)
+            nc.scalar.copy(out=values[:], in_=result[:])
+            nc.sync.dma_start(out=out_rows[:, :, cols], in_=values[:])
+            rounded = work.tile([P, BLOCK, PACK], BF16, name="rounded", tag="rounded", align_bytes=64)
+            if last:
+                nc.vector.tensor_copy(out=rounded[:], in_=values[:].rearrange("p t j -> p j t"))
+            else:
+                nc.scalar.copy(out=rounded[:], in_=result[:].rearrange("p t j -> p j t"))
+            nc.vector.quantize_mx(
+                out=out_codes[:, cols].bitcast(FP8X4), scales=out_plane[:, cols], in_=rounded[:].rearrange("p j t -> p (j t)")
+            )
+            nc.sync.dma_start(out=out_words[:, cols], in_=out_codes[:, cols].bitcast(I32))
+
+        units = [(c0, width, t) for c0, width in CHUNKS for t in range(PACK)]
+        sums_of = {}
+        pending = None
+        for c0, width, t in units:
+            if t == 0:
+                sums_of[c0] = [
+                    psum.tile([P, PACK, BLOCK], F32, name="total", tag="sum_bank", bufs=3) for b in range(width // BLOCK)
+                ]
+            fetched = work.tile([P, 4, width], F32, name="fetched", tag="fetched", align_bytes=64)
+            gather(fetched, t, c0, width, 0)
+            if pending is not None:
+                slopes(*pending)
+                if pending[2] == PACK - 1:
+                    for b, total in enumerate(pending[1]):
+                        finish(total, pending[3] + b * BLOCK)
+            for which in range(1, 4):
+                gather(fetched, t, c0, width, which)
+            pending = (fetched, sums_of[c0], t, c0, width)
+        slopes(*pending)
+        finish(pending[1][0], pending[3])
+
+        for q in range(4):
+            queue = nc.scalar if q % 2 else nc.sync
+            queue.dma_start(out=out_2[0, 4 * q : 4 * q + 4, :].bitcast(I32), in_=out_plane[32 * q : 32 * q + 4, :].bitcast(I32))

@@ -21,19 +21,20 @@ P = 128
 PACK = 4
 BLOCK = 128
 HALF = S // 2
-CHUNKS = ((0, 256), (256, 128), (384, 128))
 FLOOR = 0.05
+CHUNKS = ((0, 256), (256, 128), (384, 128))
+STEPS = len(CHUNKS) * PACK + 1
 
 
-def load_scale_rows(queue, plane, rows):
-    for q in range(4):
+def load_scale_rows(queues, plane, rows):
+    for q, queue in enumerate(queues):
         queue.dma_start(out=plane[32 * q : 32 * q + 4, :].bitcast(I32), in_=rows[4 * q : 4 * q + 4, :].bitcast(I32))
 
 
-def deal_columns(nc, dealt, raw, width):
+def deal_columns(nc, dealt, raw, width, tiles=slice(0, PACK)):
     nc.vector.tensor_copy(
-        out=dealt[:].rearrange("p (t m b) -> p t m b", t=PACK, b=width),
-        in_=raw[:].rearrange("p (m t b) -> p t m b", t=PACK, b=width),
+        out=dealt[:].rearrange("p (t m b) -> p t m b", m=P, b=width),
+        in_=raw[:].rearrange("p (m t b) -> p t m b", t=PACK, b=width)[:, tiles],
     )
 
 
@@ -44,61 +45,59 @@ def tile_picked_eikonal_none_po_kernel(
     with ExitStack() as ctx:
         keep = ctx.enter_context(tc.tile_pool(name="keep", bufs=1))
         work = ctx.enter_context(tc.tile_pool(name="work", bufs=2))
+        table = ctx.enter_context(tc.tile_pool(name="table", bufs=1))
+        late = ctx.enter_context(tc.tile_pool(name="late", bufs=1))
         psum = ctx.enter_context(tc.psum_pool(name="psum", bufs=1))
 
-        x_codes = keep.tile([P, T], U32, name="x_codes", align_bytes=64)
+        x_codes = table.tile([P, T], U32, name="x_codes", align_bytes=64, offset=0)
         x_plane = keep.tile([P, T], U8, name="x_plane", align_bytes=64)
-        w1_raw = keep.tile([P, 2 * H], U8, name="w1_raw", align_bytes=64)
-        w1_plane_raw = keep.tile([P, H], U8, name="w1_plane_raw", align_bytes=64)
-        w2_raw = keep.tile([P, 2 * N], U8, name="w2_raw", align_bytes=64)
-        w2_plane_raw = keep.tile([P, N], U8, name="w2_plane_raw", align_bytes=64)
-        gain = keep.tile([P, PACK], F32, name="gain")
+        words_raw = keep.tile([P, 2 * H], U8, name="words_raw", align_bytes=64)
+        plane_raw = keep.tile([P, H], U8, name="plane_raw", align_bytes=64)
         picks = keep.tile([P, S // 16], U16, name="picks")
-        lists = [keep.tile([P, S // 16], U16, name=name) for name in ("list_x1", "list_u1", "list_x2", "list_u2")]
+        lists = [keep.tile([P, S // 16], U16, name=name) for name in ("list_x1", "list_x2", "list_u1", "list_u2")]
         ident = keep.tile([P, P], F32, name="ident", align_bytes=64)
-        warm = keep.tile([P, 1], F32, name="warm")
+        warm = keep.tile([P, 2], F32, name="warm")
 
         nc.vector.memset(x_plane[:].bitcast(I32), 0)
-        nc.vector.memset(w1_plane_raw[:].bitcast(I32), 0)
-        nc.vector.memset(w2_plane_raw[:].bitcast(I32), 0)
+        nc.gpsimd.memset(plane_raw[:].bitcast(I32), 0)
+
+        nc.sync.dma_start(out=words_raw[:].bitcast(I32), in_=w1_words[0].bitcast(I32))
+        nc.sync.dma_start(picks[:], offs)
+        for tile, source in zip(lists, (x1, x2, u1, u2)):
+            nc.sync.dma_start(tile[:], source)
+        nc.sync.dma_start(out=x_codes[:].bitcast(I32), in_=x_words[0].rearrange("p n t -> p (n t)").bitcast(I32))
+        load_scale_rows([nc.scalar] * 4, x_plane, x_scales[0])
+        load_scale_rows([nc.gpsimd] + [nc.scalar] * 3, plane_raw, w1_scales[0])
         make_identity(nc, ident[:])
 
-        nc.sync.dma_start(out=w1_raw[:].bitcast(I32), in_=w1_words[0].bitcast(I32))
-        nc.sync.dma_start(picks[:], offs)
-        for tile, source in zip(lists, (x1, u1, x2, u2)):
-            nc.sync.dma_start(tile[:], source)
-        nc.scalar.dma_start(out=gain[:], in_=gn.rearrange("(p t) o -> p (t o)", t=PACK))
-        nc.sync.dma_start(out=x_codes[:].bitcast(I32), in_=x_words[0].rearrange("p n t -> p (n t)").bitcast(I32))
-        load_scale_rows(nc.sync, x_plane, x_scales[0])
-        load_scale_rows(nc.sync, w1_plane_raw, w1_scales[0])
-        nc.gpsimd.dma_start(out=w2_raw[:].bitcast(I32), in_=w2_words[0].bitcast(I32))
-        load_scale_rows(nc.gpsimd, w2_plane_raw, w2_scales[0])
-
-        nc.scalar.activation(out=warm[:], in_=ident[:, 0:1], func=ACT.Sqrt, bias=FLOOR)
+        nc.vector.memset(warm[:, 0:1], 1.0)
+        nc.scalar.activation(out=warm[:, 1:2], in_=warm[:, 0:1], func=ACT.Sqrt, bias=FLOOR)
 
         w1_codes = keep.tile([P, 2 * H], U8, name="w1_codes", align_bytes=64)
-        w1_plane = keep.tile([P, H], U8, name="w1_plane", align_bytes=64)
-        w2_codes = keep.tile([P, 2 * N], U8, name="w2_codes", align_bytes=64)
-        w2_plane = keep.tile([P, N], U8, name="w2_plane", align_bytes=64)
+        first_plane = keep.tile([P, P], U8, name="first_plane", align_bytes=64)
         picked_codes = keep.tile([P, S], U32, name="picked_codes", align_bytes=64)
         picked_plane = keep.tile([P, S], U8, name="picked_plane", align_bytes=64)
 
-        deal_columns(nc, w1_codes, w1_raw, 2)
+        deal_columns(nc, w1_codes, words_raw, 2)
+        nc.sync.dma_start(out=words_raw[:].bitcast(I32), in_=w2_words[0].bitcast(I32))
         nc.vector.tensor_copy(out=picked_plane[:], in_=x_plane[:].indirect(picks[:]))
-        deal_columns(nc, w1_plane, w1_plane_raw, 1)
+        deal_columns(nc, first_plane, plane_raw, 1, slice(0, 1))
         for h in range(2):
-            nc.vector.tensor_copy(
-                out=picked_codes[:, h * HALF : (h + 1) * HALF],
-                in_=x_codes[:].indirect(picks[:, h * HALF // 16 : (h + 1) * HALF // 16]),
-            )
-        deal_columns(nc, w2_codes, w2_raw, 2)
-        deal_columns(nc, w2_plane, w2_plane_raw, 1)
+            entries = picks[:, h * HALF // 16 : (h + 1) * HALF // 16]
+            nc.vector.tensor_copy(out=picked_codes[:, h * HALF : (h + 1) * HALF], in_=x_codes[:].indirect(entries))
+        rest_plane = table.tile([P, H - P], U8, name="rest_plane", align_bytes=64, offset=0)
+        deal_columns(nc, rest_plane, plane_raw, 1, slice(1, PACK))
+        w2_codes = table.tile([P, 2 * N], U8, name="w2_codes", align_bytes=64, offset=2 * H)
+        deal_columns(nc, w2_codes, words_raw, 2)
+        load_scale_rows([nc.sync] * 4, plane_raw, w2_scales[0])
+        gain = table.tile([P, PACK], F32, name="gain", align_bytes=64, offset=6 * H)
+        nc.sync.dma_start(out=gain[:], in_=gn.rearrange("(p t) o -> p (t o)", t=PACK))
 
-        def product(out, codes, plane, t, rhs, rhs_plane):
+        def product(out, codes, t, plane, rhs, rhs_plane):
             nc.tensor.matmul_mx(
                 out=out,
                 lhsT=codes[:, 2 * P * t : 2 * P * (t + 1)].bitcast(FP4X4),
-                lhsT_scale=plane[:, P * t : P * (t + 1)],
+                lhsT_scale=plane,
                 rhs=rhs.bitcast(FP8X4),
                 rhs_scale=rhs_plane,
                 start=True,
@@ -108,15 +107,12 @@ def tile_picked_eikonal_none_po_kernel(
         y = [keep.tile([P, S], F32, name=f"y{t}", align_bytes=64) for t in range(PACK)]
         for h in range(2):
             cols = slice(h * HALF, (h + 1) * HALF)
-            first = psum.tile([P, HALF], F32, name="first", tag="out_bank", bufs=2)
-            product(first[:], w1_codes, w1_plane, 0, picked_codes[:, cols], picked_plane[:, cols])
-            if h == 0:
-                nc.scalar.copy(out=y[0][:, cols], in_=first[:])
-            else:
-                nc.vector.tensor_copy(out=y[0][:, cols], in_=first[:])
+            first = psum.tile([P, HALF], F32, name="first", tag="out_bank", bufs=3)
+            product(first[:], w1_codes, 0, first_plane[:], picked_codes[:, cols], picked_plane[:, cols])
+            nc.scalar.copy(out=y[0][:, cols], in_=first[:])
         for t in range(1, PACK):
             bank = psum.tile([P, S], F32, name="bank", tag="sum_bank", bufs=3)
-            product(bank[:], w1_codes, w1_plane, t, picked_codes[:], picked_plane[:])
+            product(bank[:], w1_codes, t, rest_plane[:, P * (t - 1) : P * t], picked_codes[:], picked_plane[:])
             nc.scalar.copy(out=y[t][:], in_=bank[:])
 
         out_codes = keep.tile([P, S], U32, name="out_codes", align_bytes=64)
@@ -124,89 +120,130 @@ def tile_picked_eikonal_none_po_kernel(
         out_rows = out_0.rearrange("(p t) j -> p t j", t=PACK)
         out_words = out_1[0].rearrange("p n t -> p (n t)").bitcast(I32)
 
-        def gather(fetched, t, c0, width, which):
+        z_rows = keep.tile([P, PACK, HALF], BF16, name="z_rows", align_bytes=64)
+        roots = {b: keep.tile([P, BLOCK, PACK], F32, name=f"root{b}", align_bytes=64) for b in (2, 3)}
+        z = [keep.tile([P, BLOCK, PACK], BF16, name=f"z{b}", align_bytes=64) for b in range(S // BLOCK)]
+
+        def interleave(copy, b):
+            copy(out=z[b][:], in_=z_rows[:, :, b * BLOCK : (b + 1) * BLOCK].rearrange("p t j -> p j t"))
+
+        def gather(fetched, step, n):
+            c0, width, t, sides = step
+            which, k = divmod(n, len(sides))
             nc.vector.tensor_scalar(
-                out=fetched[:, which, :],
-                in0=y[t][:].indirect(lists[which][:, c0 // 16 : (c0 + width) // 16]),
+                out=fetched[:, which, k, :],
+                in0=y[t][:].indirect(lists[2 * sides[k] + which][:, c0 // 16 : (c0 + width) // 16]),
                 scalar1=-1.0,
                 scalar2=0.0,
                 op0=ALU.mult,
                 op1=ALU.add,
             )
 
-        def slopes(fetched, sums, t, c0, width):
+        def slopes(fetched, total, step):
+            c0, width, t, sides = step
             blocks = width // BLOCK
-            least = work.tile([P, 2, width], F32, name="least", tag="least", align_bytes=64)
-            nc.vector.tensor_tensor(out=least[:], in0=fetched[:, 0:2, :], in1=fetched[:, 2:4, :], op=ALU.max)
-            diff = psum.tile([P, 2, blocks, P], F32, name="diff", tag="diff_bank", bufs=3)
-            for side in range(2):
+            least = work.tile([P, len(sides), width], F32, name="least", tag="least", bufs=STEPS, align_bytes=64)
+            nc.vector.tensor_tensor(out=least[:], in0=fetched[:, 0], in1=fetched[:, 1], op=ALU.max)
+            diff = psum.tile([P, len(sides), blocks, P], F32, name="diff", tag="diff_bank", bufs=2)
+            for k in range(len(sides)):
                 for b in range(blocks):
                     cols = slice(c0 + b * BLOCK, c0 + (b + 1) * BLOCK)
-                    nc.tensor.matmul(diff[:, side, b, :], lhsT=y[t][:, cols], rhs=ident[:], start=True, stop=False, is_transpose=True)
+                    nc.tensor.matmul(diff[:, k, b, :], lhsT=y[t][:, cols], rhs=ident[:], start=True, stop=False, is_transpose=True)
                     nc.tensor.matmul(
-                        diff[:, side, b, :],
-                        lhsT=least[:, side, b * BLOCK : (b + 1) * BLOCK],
+                        diff[:, k, b, :],
+                        lhsT=least[:, k, b * BLOCK : (b + 1) * BLOCK],
                         rhs=ident[:],
                         start=False,
                         stop=True,
                         is_transpose=True,
                     )
-            rise = work.tile([P, 2, blocks, P], F32, name="rise", tag="rise", align_bytes=64)
+            rise = work.tile([P, len(sides), blocks, P], F32, name="rise", tag="rise", align_bytes=64)
             nc.scalar.activation(out=rise[:], in_=diff[:], func=ACT.Relu)
-            square = work.tile([P, 2, blocks, P], F32, name="square", tag="square", align_bytes=64)
+            square = work.tile([P, len(sides), blocks, P], F32, name="square", tag="square", align_bytes=64)
             nc.scalar.activation(out=square[:], in_=rise[:], func=ACT.Square)
             for b in range(blocks):
-                for side in range(2):
+                for k, side in enumerate(sides):
                     nc.tensor.matmul(
-                        sums[b][:, t, :], lhsT=square[:, side, b, :], rhs=ident[:], start=side == 0, stop=side == 1, is_transpose=True
+                        total[:, b if c0 == 0 else t, :],
+                        lhsT=square[:, k, b, :],
+                        rhs=ident[:],
+                        start=side == 0,
+                        stop=side == 1,
+                        is_transpose=True,
                     )
+            if c0 == 0:
+                root = work.tile([P, width], F32, name="root", tag="root", align_bytes=64)
+                nc.scalar.activation(out=root[:], in_=total[:].rearrange("p b j -> p (b j)"), func=ACT.Sqrt, bias=FLOOR)
+                nc.scalar.activation(out=z_rows[:, t, :], in_=root[:], func=ACT.Copy, scale=gain[:, t : t + 1])
+                if t == PACK - 1:
+                    for b in range(blocks):
+                        interleave(nc.scalar.copy, b)
+            elif t == PACK - 1 and sides[-1] == 1:
+                nc.scalar.activation(
+                    out=roots[c0 // BLOCK][:], in_=total[:].rearrange("p t j -> p j t"), func=ACT.Sqrt, bias=FLOOR
+                )
 
-        def finish(total, c0):
-            cols = slice(c0, c0 + BLOCK)
-            last = c0 + BLOCK == S
-            root = work.tile([P, BLOCK, PACK], F32, name="root", tag="root", align_bytes=64)
-            nc.scalar.activation(out=root[:], in_=total[:].rearrange("p t j -> p j t"), func=ACT.Sqrt, bias=FLOOR)
-            z = work.tile([P, BLOCK, PACK], BF16, name="z", tag="z", align_bytes=64)
-            nc.vector.tensor_tensor(out=z[:], in0=root[:], in1=gain[:].unsqueeze(1).to_broadcast([P, BLOCK, PACK]), op=ALU.mult)
-            z_codes = work.tile([P, BLOCK], U32, name="z_codes", tag="z_codes", align_bytes=64)
+        def finish(b):
+            cols = slice(b * BLOCK, (b + 1) * BLOCK)
+            if b in roots:
+                nc.vector.tensor_tensor(
+                    out=z[b][:], in0=roots[b][:], in1=gain[:].unsqueeze(1).to_broadcast([P, BLOCK, PACK]), op=ALU.mult
+                )
+            z_codes = work.tile([P, BLOCK], U32, name="z_codes", tag="square", align_bytes=64)
             z_plane = work.tile([P, BLOCK], U8, name="z_plane", tag="z_plane", align_bytes=64)
-            nc.vector.quantize_mx(out=z_codes[:].bitcast(FP8X4), scales=z_plane[:], in_=z[:].rearrange("p j t -> p (j t)"))
-            result = psum.tile([P, PACK, BLOCK], F32, name="result", tag="out_bank", bufs=2)
-            for t in range(PACK):
-                product(result[:, t, :], w2_codes, w2_plane, t, z_codes[:], z_plane[:])
-            values = work.tile([P, PACK, BLOCK], F32, name="values", tag="values", align_bytes=64)
-            nc.scalar.copy(out=values[:], in_=result[:])
-            nc.sync.dma_start(out=out_rows[:, :, cols], in_=values[:])
-            rounded = work.tile([P, BLOCK, PACK], BF16, name="rounded", tag="rounded", align_bytes=64)
-            if last:
-                nc.vector.tensor_copy(out=rounded[:], in_=values[:].rearrange("p t j -> p j t"))
+            nc.vector.quantize_mx(out=z_codes[:].bitcast(FP8X4), scales=z_plane[:], in_=z[b][:].rearrange("p j t -> p (j t)"))
+            values = work.tile([P, PACK, BLOCK], F32, name="values", tag="values", bufs=4, align_bytes=64)
+            if b == S // BLOCK - 1:
+                for pair, copy in enumerate((nc.scalar.copy, nc.vector.tensor_copy)):
+                    result = psum.tile([P, 2, BLOCK], F32, name="result", tag="out_bank", bufs=3)
+                    for k in range(2):
+                        t = 2 * pair + k
+                        product(result[:, k, :], w2_codes, t, w2_plane[:, P * t : P * (t + 1)], z_codes[:], z_plane[:])
+                    copy(out=values[:, 2 * pair : 2 * pair + 2, :], in_=result[:])
             else:
-                nc.scalar.copy(out=rounded[:], in_=result[:].rearrange("p t j -> p j t"))
+                result = psum.tile([P, PACK, BLOCK], F32, name="result", tag="out_bank", bufs=3)
+                for t in range(PACK):
+                    product(result[:, t, :], w2_codes, t, w2_plane[:, P * t : P * (t + 1)], z_codes[:], z_plane[:])
+                nc.scalar.copy(out=values[:], in_=result[:])
+            nc.sync.dma_start(out=out_rows[:, :, cols], in_=values[:])
+            return values
+
+        def hand_on(b, values):
+            cols = slice(b * BLOCK, (b + 1) * BLOCK)
+            rounded = work.tile([P, BLOCK, PACK], BF16, name="rounded", tag="rounded", align_bytes=64)
+            nc.vector.tensor_copy(out=rounded[:], in_=values[:].rearrange("p t j -> p j t"))
             nc.vector.quantize_mx(
                 out=out_codes[:, cols].bitcast(FP8X4), scales=out_plane[:, cols], in_=rounded[:].rearrange("p j t -> p (j t)")
             )
-            nc.sync.dma_start(out=out_words[:, cols], in_=out_codes[:, cols].bitcast(I32))
 
-        units = [(c0, width, t) for c0, width in CHUNKS for t in range(PACK)]
-        sums_of = {}
+        steps = [(c0, width, t, (0, 1)) for c0, width in CHUNKS for t in range(PACK)]
+        c0, width, t, sides = steps.pop()
+        steps.extend((c0, width, t, (side,)) for side in sides)
         pending = None
-        for c0, width, t in units:
-            if t == 0:
-                sums_of[c0] = [
-                    psum.tile([P, PACK, BLOCK], F32, name="total", tag="sum_bank", bufs=3) for b in range(width // BLOCK)
-                ]
-            fetched = work.tile([P, 4, width], F32, name="fetched", tag="fetched", align_bytes=64)
-            gather(fetched, t, c0, width, 0)
+        for step in steps:
+            c0, width, t, sides = step
+            if c0 == 0:
+                total = psum.tile([P, width // BLOCK, BLOCK], F32, name="total", tag="sum_bank", bufs=3)
+            elif t == 0:
+                total = psum.tile([P, PACK, BLOCK], F32, name="total", tag="sum_bank", bufs=3)
+            if step == steps[-1]:
+                fetched = late.tile([P, 2, 1, width], F32, name="fetched_last", align_bytes=64, offset=0)
+            else:
+                fetched = work.tile([P, 2, len(sides), width], F32, name="fetched", tag="fetched", bufs=STEPS, align_bytes=64)
+            gather(fetched, step, 0)
             if pending is not None:
                 slopes(*pending)
-                if pending[2] == PACK - 1:
-                    for b, total in enumerate(pending[1]):
-                        finish(total, pending[3] + b * BLOCK)
-            for which in range(1, 4):
-                gather(fetched, t, c0, width, which)
-            pending = (fetched, sums_of[c0], t, c0, width)
+            for n in range(1, 2 * len(sides)):
+                gather(fetched, step, n)
+            pending = (fetched, total, step)
         slopes(*pending)
-        finish(pending[1][0], pending[3])
+        w2_plane = late.tile([P, N], U8, name="w2_plane", align_bytes=64, offset=0)
+        deal_columns(nc, w2_plane, plane_raw, 1)
+        results = [finish(b) for b in range(S // BLOCK)]
+        for b, values in enumerate(results):
+            hand_on(b, values)
+        for cols in (slice(0, S - BLOCK), slice(S - BLOCK, S)):
+            nc.scalar.dma_start(out=out_words[:, cols], in_=out_codes[:, cols].bitcast(I32))
 
         for q in range(4):
             queue = nc.scalar if q % 2 else nc.sync

from contextlib import ExitStack

import concourse.mybir as mybir
from concourse.masks import make_identity

K, T, S, H, N = 512, 2048, 512, 512, 512
FLOPS = 2 * K * H * S + 2 * H * N * S

F32 = mybir.dt.float32
BF16 = mybir.dt.bfloat16
I32 = mybir.dt.int32
U32 = mybir.dt.uint32
U16 = mybir.dt.uint16
U8 = mybir.dt.uint8
FP8X4 = mybir.dt.float8_e4m3fn_x4
FP4X4 = mybir.dt.float4_e2m1fn_x4
ALU = mybir.AluOpType
ACT = mybir.ActivationFunctionType

P = 128
PACK = 4
BLOCK = 128
HALF = S // 2
FLOOR = 0.05
CHUNKS = ((0, 256), (256, 128), (384, 128))
STEPS = len(CHUNKS) * PACK + 1


def load_scale_rows(queues, plane, rows):
    for q, queue in enumerate(queues):
        queue.dma_start(out=plane[32 * q : 32 * q + 4, :].bitcast(I32), in_=rows[4 * q : 4 * q + 4, :].bitcast(I32))


def deal_columns(nc, dealt, raw, width, tiles=slice(0, PACK)):
    nc.vector.tensor_copy(
        out=dealt[:].rearrange("p (t m b) -> p t m b", m=P, b=width),
        in_=raw[:].rearrange("p (m t b) -> p t m b", t=PACK, b=width)[:, tiles],
    )


def tile_picked_eikonal_none_po_kernel(
    tc, x_words, x_scales, w1_words, w1_scales, gn, w2_words, w2_scales, offs, x1, x2, u1, u2, out_0, out_1, out_2
):
    nc = tc.nc
    with ExitStack() as ctx:
        keep = ctx.enter_context(tc.tile_pool(name="keep", bufs=1))
        work = ctx.enter_context(tc.tile_pool(name="work", bufs=2))
        table = ctx.enter_context(tc.tile_pool(name="table", bufs=1))
        late = ctx.enter_context(tc.tile_pool(name="late", bufs=1))
        psum = ctx.enter_context(tc.psum_pool(name="psum", bufs=1))

        x_codes = table.tile([P, T], U32, name="x_codes", align_bytes=64, offset=0)
        x_plane = keep.tile([P, T], U8, name="x_plane", align_bytes=64)
        words_raw = keep.tile([P, 2 * H], U8, name="words_raw", align_bytes=64)
        plane_raw = keep.tile([P, H], U8, name="plane_raw", align_bytes=64)
        picks = keep.tile([P, S // 16], U16, name="picks")
        lists = [keep.tile([P, S // 16], U16, name=name) for name in ("list_x1", "list_x2", "list_u1", "list_u2")]
        ident = keep.tile([P, P], F32, name="ident", align_bytes=64)
        warm = keep.tile([P, 2], F32, name="warm")

        nc.vector.memset(x_plane[:].bitcast(I32), 0)
        nc.gpsimd.memset(plane_raw[:].bitcast(I32), 0)

        nc.sync.dma_start(out=words_raw[:].bitcast(I32), in_=w1_words[0].bitcast(I32))
        nc.sync.dma_start(picks[:], offs)
        for tile, source in zip(lists, (x1, x2, u1, u2)):
            nc.sync.dma_start(tile[:], source)
        nc.sync.dma_start(out=x_codes[:].bitcast(I32), in_=x_words[0].rearrange("p n t -> p (n t)").bitcast(I32))
        load_scale_rows([nc.scalar] * 4, x_plane, x_scales[0])
        load_scale_rows([nc.gpsimd] + [nc.scalar] * 3, plane_raw, w1_scales[0])
        make_identity(nc, ident[:])

        nc.vector.memset(warm[:, 0:1], 1.0)
        nc.scalar.activation(out=warm[:, 1:2], in_=warm[:, 0:1], func=ACT.Sqrt, bias=FLOOR)

        w1_codes = keep.tile([P, 2 * H], U8, name="w1_codes", align_bytes=64)
        first_plane = keep.tile([P, P], U8, name="first_plane", align_bytes=64)
        picked_codes = keep.tile([P, S], U32, name="picked_codes", align_bytes=64)
        picked_plane = keep.tile([P, S], U8, name="picked_plane", align_bytes=64)

        deal_columns(nc, w1_codes, words_raw, 2)
        nc.sync.dma_start(out=words_raw[:].bitcast(I32), in_=w2_words[0].bitcast(I32))
        nc.vector.tensor_copy(out=picked_plane[:], in_=x_plane[:].indirect(picks[:]))
        deal_columns(nc, first_plane, plane_raw, 1, slice(0, 1))
        for h in range(2):
            entries = picks[:, h * HALF // 16 : (h + 1) * HALF // 16]
            nc.vector.tensor_copy(out=picked_codes[:, h * HALF : (h + 1) * HALF], in_=x_codes[:].indirect(entries))
        rest_plane = table.tile([P, H - P], U8, name="rest_plane", align_bytes=64, offset=0)
        deal_columns(nc, rest_plane, plane_raw, 1, slice(1, PACK))
        w2_codes = table.tile([P, 2 * N], U8, name="w2_codes", align_bytes=64, offset=2 * H)
        deal_columns(nc, w2_codes, words_raw, 2)
        load_scale_rows([nc.sync] * 4, plane_raw, w2_scales[0])
        gain = table.tile([P, PACK], F32, name="gain", align_bytes=64, offset=6 * H)
        nc.sync.dma_start(out=gain[:], in_=gn.rearrange("(p t) o -> p (t o)", t=PACK))

        def product(out, codes, t, plane, rhs, rhs_plane):
            nc.tensor.matmul_mx(
                out=out,
                lhsT=codes[:, 2 * P * t : 2 * P * (t + 1)].bitcast(FP4X4),
                lhsT_scale=plane,
                rhs=rhs.bitcast(FP8X4),
                rhs_scale=rhs_plane,
                start=True,
                stop=True,
            )

        y = [keep.tile([P, S], F32, name=f"y{t}", align_bytes=64) for t in range(PACK)]
        for h in range(2):
            cols = slice(h * HALF, (h + 1) * HALF)
            first = psum.tile([P, HALF], F32, name="first", tag="out_bank", bufs=3)
            product(first[:], w1_codes, 0, first_plane[:], picked_codes[:, cols], picked_plane[:, cols])
            nc.scalar.copy(out=y[0][:, cols], in_=first[:])
        for t in range(1, PACK):
            bank = psum.tile([P, S], F32, name="bank", tag="sum_bank", bufs=3)
            product(bank[:], w1_codes, t, rest_plane[:, P * (t - 1) : P * t], picked_codes[:], picked_plane[:])
            nc.scalar.copy(out=y[t][:], in_=bank[:])

        out_codes = keep.tile([P, S], U32, name="out_codes", align_bytes=64)
        out_plane = keep.tile([P, S], U8, name="out_plane", align_bytes=64)
        out_rows = out_0.rearrange("(p t) j -> p t j", t=PACK)
        out_words = out_1[0].rearrange("p n t -> p (n t)").bitcast(I32)

        z_rows = keep.tile([P, PACK, HALF], BF16, name="z_rows", align_bytes=64)
        roots = {b: keep.tile([P, BLOCK, PACK], F32, name=f"root{b}", align_bytes=64) for b in (2, 3)}
        z = [keep.tile([P, BLOCK, PACK], BF16, name=f"z{b}", align_bytes=64) for b in range(S // BLOCK)]

        def interleave(copy, b):
            copy(out=z[b][:], in_=z_rows[:, :, b * BLOCK : (b + 1) * BLOCK].rearrange("p t j -> p j t"))

        def gather(fetched, step, n):
            c0, width, t, sides = step
            which, k = divmod(n, len(sides))
            nc.vector.tensor_scalar(
                out=fetched[:, which, k, :],
                in0=y[t][:].indirect(lists[2 * sides[k] + which][:, c0 // 16 : (c0 + width) // 16]),
                scalar1=-1.0,
                scalar2=0.0,
                op0=ALU.mult,
                op1=ALU.add,
            )

        def slopes(fetched, total, step):
            c0, width, t, sides = step
            blocks = width // BLOCK
            least = work.tile([P, len(sides), width], F32, name="least", tag="least", bufs=STEPS, align_bytes=64)
            nc.vector.tensor_tensor(out=least[:], in0=fetched[:, 0], in1=fetched[:, 1], op=ALU.max)
            diff = psum.tile([P, len(sides), blocks, P], F32, name="diff", tag="diff_bank", bufs=2)
            for k in range(len(sides)):
                for b in range(blocks):
                    cols = slice(c0 + b * BLOCK, c0 + (b + 1) * BLOCK)
                    nc.tensor.matmul(diff[:, k, b, :], lhsT=y[t][:, cols], rhs=ident[:], start=True, stop=False, is_transpose=True)
                    nc.tensor.matmul(
                        diff[:, k, b, :],
                        lhsT=least[:, k, b * BLOCK : (b + 1) * BLOCK],
                        rhs=ident[:],
                        start=False,
                        stop=True,
                        is_transpose=True,
                    )
            rise = work.tile([P, len(sides), blocks, P], F32, name="rise", tag="rise", align_bytes=64)
            nc.scalar.activation(out=rise[:], in_=diff[:], func=ACT.Relu)
            square = work.tile([P, len(sides), blocks, P], F32, name="square", tag="square", align_bytes=64)
            nc.scalar.activation(out=square[:], in_=rise[:], func=ACT.Square)
            for b in range(blocks):
                for k, side in enumerate(sides):
                    nc.tensor.matmul(
                        total[:, b if c0 == 0 else t, :],
                        lhsT=square[:, k, b, :],
                        rhs=ident[:],
                        start=side == 0,
                        stop=side == 1,
                        is_transpose=True,
                    )
            if c0 == 0:
                root = work.tile([P, width], F32, name="root", tag="root", align_bytes=64)
                nc.scalar.activation(out=root[:], in_=total[:].rearrange("p b j -> p (b j)"), func=ACT.Sqrt, bias=FLOOR)
                nc.scalar.activation(out=z_rows[:, t, :], in_=root[:], func=ACT.Copy, scale=gain[:, t : t + 1])
                if t == PACK - 1:
                    for b in range(blocks):
                        interleave(nc.scalar.copy, b)
            elif t == PACK - 1 and sides[-1] == 1:
                nc.scalar.activation(
                    out=roots[c0 // BLOCK][:], in_=total[:].rearrange("p t j -> p j t"), func=ACT.Sqrt, bias=FLOOR
                )

        def finish(b):
            cols = slice(b * BLOCK, (b + 1) * BLOCK)
            if b in roots:
                nc.vector.tensor_tensor(
                    out=z[b][:], in0=roots[b][:], in1=gain[:].unsqueeze(1).to_broadcast([P, BLOCK, PACK]), op=ALU.mult
                )
            z_codes = work.tile([P, BLOCK], U32, name="z_codes", tag="square", align_bytes=64)
            z_plane = work.tile([P, BLOCK], U8, name="z_plane", tag="z_plane", align_bytes=64)
            nc.vector.quantize_mx(out=z_codes[:].bitcast(FP8X4), scales=z_plane[:], in_=z[b][:].rearrange("p j t -> p (j t)"))
            values = work.tile([P, PACK, BLOCK], F32, name="values", tag="values", bufs=4, align_bytes=64)
            if b == S // BLOCK - 1:
                for pair, copy in enumerate((nc.scalar.copy, nc.vector.tensor_copy)):
                    result = psum.tile([P, 2, BLOCK], F32, name="result", tag="out_bank", bufs=3)
                    for k in range(2):
                        t = 2 * pair + k
                        product(result[:, k, :], w2_codes, t, w2_plane[:, P * t : P * (t + 1)], z_codes[:], z_plane[:])
                    copy(out=values[:, 2 * pair : 2 * pair + 2, :], in_=result[:])
            else:
                result = psum.tile([P, PACK, BLOCK], F32, name="result", tag="out_bank", bufs=3)
                for t in range(PACK):
                    product(result[:, t, :], w2_codes, t, w2_plane[:, P * t : P * (t + 1)], z_codes[:], z_plane[:])
                nc.scalar.copy(out=values[:], in_=result[:])
            nc.sync.dma_start(out=out_rows[:, :, cols], in_=values[:])
            return values

        def hand_on(b, values):
            cols = slice(b * BLOCK, (b + 1) * BLOCK)
            rounded = work.tile([P, BLOCK, PACK], BF16, name="rounded", tag="rounded", align_bytes=64)
            nc.vector.tensor_copy(out=rounded[:], in_=values[:].rearrange("p t j -> p j t"))
            nc.vector.quantize_mx(
                out=out_codes[:, cols].bitcast(FP8X4), scales=out_plane[:, cols], in_=rounded[:].rearrange("p j t -> p (j t)")
            )

        steps = [(c0, width, t, (0, 1)) for c0, width in CHUNKS for t in range(PACK)]
        c0, width, t, sides = steps.pop()
        steps.extend((c0, width, t, (side,)) for side in sides)
        pending = None
        for step in steps:
            c0, width, t, sides = step
            if c0 == 0:
                total = psum.tile([P, width // BLOCK, BLOCK], F32, name="total", tag="sum_bank", bufs=3)
            elif t == 0:
                total = psum.tile([P, PACK, BLOCK], F32, name="total", tag="sum_bank", bufs=3)
            if step == steps[-1]:
                fetched = late.tile([P, 2, 1, width], F32, name="fetched_last", align_bytes=64, offset=0)
            else:
                fetched = work.tile([P, 2, len(sides), width], F32, name="fetched", tag="fetched", bufs=STEPS, align_bytes=64)
            gather(fetched, step, 0)
            if pending is not None:
                slopes(*pending)
            for n in range(1, 2 * len(sides)):
                gather(fetched, step, n)
            pending = (fetched, total, step)
        slopes(*pending)
        w2_plane = late.tile([P, N], U8, name="w2_plane", align_bytes=64, offset=0)
        deal_columns(nc, w2_plane, plane_raw, 1)
        results = [finish(b) for b in range(S // BLOCK)]
        for b, values in enumerate(results):
            hand_on(b, values)
        for cols in (slice(0, S - BLOCK), slice(S - BLOCK, S)):
            nc.scalar.dma_start(out=out_words[:, cols], in_=out_codes[:, cols].bitcast(I32))

        for q in range(4):
            queue = nc.scalar if q % 2 else nc.sync
            queue.dma_start(out=out_2[0, 4 * q : 4 * q + 4, :].bitcast(I32), in_=out_plane[32 * q : 32 * q + 4, :].bitcast(I32))
